import numpy as np
import ml_dtypes


def mxq(x, axis, fmt="e4m3"):
    dtype, down = {"e4m3": (ml_dtypes.float8_e4m3fn, 7), "e5m2": (ml_dtypes.float8_e5m2, 14)}[fmt]
    v = np.moveaxis(np.asarray(x, np.float32).astype(ml_dtypes.bfloat16).astype(np.float64), axis, -1)
    blocks = v.reshape(v.shape[:-1] + (-1, 32))
    amax = np.abs(blocks).max(-1, keepdims=True)
    byte = np.maximum(np.where(amax > 0, np.frexp(amax)[1] - 1 + 127, 0) - down, 1)
    scale = np.exp2(byte - 127.0)
    codes = (blocks / scale).astype(np.float32).astype(dtype).astype(np.float64)
    return np.moveaxis((codes * scale).reshape(v.shape), -1, axis)


WIDE = False


def mx_kscale(k):
    if not WIDE:
        return np.ones(k)
    levels = np.array([30, -30])
    if k % 512:
        return np.exp2(np.random.permutation(np.resize(levels, k // 32))).repeat(32)
    a = np.empty((k // 512, 16))
    for p in range(k // 512):
        a[p, :8] = np.random.permutation(np.resize(levels, 8))
        for g in range(8):
            far = levels[np.abs(levels - a[p, g]) >= 10]
            a[p, g + 8] = far[np.random.randint(len(far))]
    return np.exp2(a.ravel()).repeat(32)


def f64(x):
    return np.asarray(x).astype(np.float64)


def striped(idx):
    return np.tile(np.asarray(idx).reshape(-1, 16).T, (8, 1)).astype(np.uint16)


def unstriped(offs):
    return offs[:16].T.reshape(-1).astype(np.int64)


E2M1 = np.array([0.0, 0.5, 1.0, 1.5, 2.0, 3.0, 4.0, 6.0, -0.0, -0.5, -1.0, -1.5, -2.0, -3.0, -4.0, -6.0])


def pack_weight(w, fmt):
    k, n = w.shape
    w = f64(np.asarray(w, np.float32).astype(ml_dtypes.bfloat16)).reshape(k // 32, 32, n)
    amax = np.abs(w).max(1)
    if fmt in ("e4m3", "e5m2"):
        byte = np.frexp(amax)[1] - 1 + 127 - (7 if fmt == "e4m3" else 14)
    else:
        mant, ex = np.frexp(amax / 6.0)
        byte = np.where(mant > 0.5, ex, ex - 1) + 127
    byte = np.clip(np.where(amax > 0, byte, 1), 1, 254)
    scaled = (w * np.exp2(127.0 - byte)[:, None, :]).reshape(k, n).astype(np.float32)
    by_word = np.ascontiguousarray(scaled.reshape(k // 512, 128, 4, n).transpose(0, 1, 3, 2))
    if fmt in ("e4m3", "e5m2"):
        words = by_word.astype(ml_dtypes.float8_e4m3fn if fmt == "e4m3" else ml_dtypes.float8_e5m2).view(np.uint8)
    else:
        c = by_word.astype(ml_dtypes.float4_e2m1fn).view(np.uint8) & 0xF
        words = (c[..., 0::2] | (c[..., 1::2] << 4)).reshape(k // 512, 128, 2 * n)
    return np.ascontiguousarray(words), np.ascontiguousarray(byte.astype(np.uint8).reshape(k // 512, 16, n))


def unpack_weight(words, scales, fmt):
    g, _, n = scales.shape
    words = np.ascontiguousarray(words).reshape(g, 128, n, -1)
    if fmt in ("e4m3", "e5m2"):
        vals = words.view(ml_dtypes.float8_e4m3fn if fmt == "e4m3" else ml_dtypes.float8_e5m2).astype(np.float64)
    else:
        nib = np.empty((g, 128, n, 4), np.uint8)
        nib[..., 0::2] = words & 0xF
        nib[..., 1::2] = words >> 4
        vals = E2M1[nib]
    vals = vals * np.repeat(np.exp2(scales.astype(np.float64) - 127.0), 8, axis=1)[..., None]
    return vals.transpose(0, 1, 3, 2).reshape(g * 512, n)


K, T, J, I, R = 512, 512, 256, 256, 512


def setup_inputs():
    n = np.random.standard_normal
    idx = np.random.permutation(T)[:J]
    idx2 = np.random.permutation(T)[:I]
    fk = mx_kscale(K)
    fr = mx_kscale(R)
    xtp = pack_weight(n((K, T)) / fk[:, None], "e4m3")
    wap = pack_weight(n((K, R)) * 0.5 / np.sqrt(K) * fk[:, None] * fr, "e5m2")
    wbp = pack_weight(n((K, R)) * 1 / np.sqrt(K) * fk[:, None] / fr, "e2m1")
    return {
        "xt_words": xtp[0],
        "xt_scales": xtp[1],
        "wa_words": wap[0],
        "wa_scales": wap[1],
        "wb_words": wbp[0],
        "wb_scales": wbp[1],
        "tg": (np.random.uniform(-10.0, 20.0, (J, 1))).astype(np.float32),
        "cw1": (np.random.uniform(0.5, 2.0, (1, I))).astype(np.float32),
        "offs": striped(idx),
        "offs2": striped(idx2),
    }


def reference(xt_words, xt_scales, wa_words, wa_scales, wb_words, wb_scales, tg, cw1, offs, offs2):
    idx = unstriped(offs)
    idx2 = unstriped(offs2)
    xtu = unpack_weight(xt_words, xt_scales, "e4m3")
    wau = unpack_weight(wa_words, wa_scales, "e5m2")
    wbu = unpack_weight(wb_words, wb_scales, "e2m1")
    xtidxg = xtu[:, idx]
    za = wau.T @ xtidxg
    ka1 = np.max(za, axis=1, keepdims=True)
    ha = np.maximum(za - 0.4 * ka1, 0.0)
    xtidx2g = xtu[:, idx2]
    zb = wbu.T @ xtidx2g
    hb = np.maximum(zb, 0.0)
    haq = mxq(ha, 0, "e4m3")
    hbq = mxq(hb, 0, "e5m2")
    a0 = haq.T @ hbq
    y = 0.04 * np.maximum(a0 - f64(tg), 0.0) * f64(cw1)
    return y

@@ -1,0 +1,189 @@
+from contextlib import ExitStack
+
+import concourse.mybir as mybir
+
+K, T, J, I, R = 512, 512, 256, 256, 512
+FLOPS = 2 * K * R * J + 2 * K * R * I + 2 * R * J * I
+
+F32 = mybir.dt.float32
+BF16 = mybir.dt.bfloat16
+I32 = mybir.dt.int32
+U32 = mybir.dt.uint32
+U16 = mybir.dt.uint16
+U8 = mybir.dt.uint8
+E4M3 = mybir.dt.float8_e4m3fn_x4
+E5M2 = mybir.dt.float8_e5m2_x4
+E2M1 = mybir.dt.float4_e2m1fn_x4
+ALU = mybir.AluOpType
+RELU = mybir.ActivationFunctionType.Relu
+AXIS_X = mybir.AxisListType.X
+
+P = 128
+
+
+def load_scales(queues, plane, scales):
+    for q in range(4):
+        queues[q].dma_start(
+            out=plane[32 * q : 32 * q + 4, :].bitcast(I32),
+            in_=scales[0, 4 * q : 4 * q + 4, :].bitcast(I32),
+        )
+
+
+def deal(engine_copy, dealt, raw):
+    engine_copy(
+        out=dealt.rearrange("p (t b q) -> p t b q", t=4, b=16),
+        in_=raw.rearrange("p (b t q) -> p t b q", t=4, b=16),
+    )
+
+
+def tile_list_meet_peakgated_plain_hinge_kernel(
+    tc, xt_words, xt_scales, wa_words, wa_scales, wb_words, wb_scales, tg, cw1, offs, offs2, out
+):
+    nc = tc.nc
+    with ExitStack() as ctx:
+        pool = ctx.enter_context(tc.tile_pool(name="keep", bufs=1))
+        psum = ctx.enter_context(tc.psum_pool(name="psum", bufs=1))
+
+        def tile(shape, dtype, name):
+            return pool.tile(shape, dtype, name=name, align_bytes=64)
+
+        list_a = pool.tile([P, J // 16], U16, name="list_a")
+        list_b = pool.tile([P, I // 16], U16, name="list_b")
+        x_words = tile([P, T], U32, "x_words")
+        x_scales = tile([P, T], U8, "x_scales")
+        wa_raw = tile([P, R], U32, "wa_raw")
+        wa_scales_raw = tile([P, R], U8, "wa_scales_raw")
+        wb_raw = tile([P, R // 2], U32, "wb_raw")
+        wb_scales_raw = tile([P, R], U8, "wb_scales_raw")
+        target = tile([P, 2], F32, "target")
+        col_weight = tile([P, I], F32, "col_weight")
+
+        nc.vector.memset(x_scales[:].bitcast(I32), 0)
+        nc.vector.memset(wa_scales_raw[:].bitcast(I32), 0)
+        nc.vector.memset(wb_scales_raw[:].bitcast(I32), 0)
+
+        nc.sync.dma_start(list_a[:], offs)
+        nc.sync.dma_start(
+            out=x_words[:].bitcast(I32), in_=xt_words[0].rearrange("p n t -> p (n t)").bitcast(I32)
+        )
+        nc.scalar.dma_start(
+            out=wa_raw[:].bitcast(I32), in_=wa_words[0].rearrange("p n t -> p (n t)").bitcast(I32)
+        )
+        load_scales([nc.sync] * 4, x_scales, xt_scales)
+        nc.sync.dma_start(list_b[:], offs2)
+        load_scales([nc.sync] * 4, wa_scales_raw, wa_scales)
+        nc.sync.dma_start(out=wb_raw[:].bitcast(I32), in_=wb_words[0].bitcast(I32))
+        load_scales([nc.sync, nc.sync, nc.sync, nc.gpsimd], wb_scales_raw, wb_scales)
+        with nc.allow_non_contiguous_dma(reason="one target for each partition"):
+            nc.sync.dma_start(out=target[:], in_=tg.rearrange("(h p) o -> p (h o)", p=P))
+        nc.sync.dma_start(out=col_weight[:], in_=cw1[0].partition_broadcast(P))
+
+        wa_dealt = tile([P, R], U32, "wa_dealt")
+        wa_scales_dealt = tile([P, R], U8, "wa_scales_dealt")
+        wb_dealt = tile([P, 2 * R], U8, "wb_dealt")
+        wb_scales_dealt = tile([P, R], U8, "wb_scales_dealt")
+        deal(nc.scalar.copy, wa_dealt[:], wa_raw[:])
+        deal(nc.scalar.copy, wa_scales_dealt[:].bitcast(U32), wa_scales_raw[:].bitcast(U32))
+        deal(nc.scalar.copy, wb_dealt[:].bitcast(U32), wb_raw[:])
+        deal(nc.scalar.copy, wb_scales_dealt[:].bitcast(U32), wb_scales_raw[:].bitcast(U32))
+
+        neg_target = tile([P, 2], F32, "neg_target")
+        nc.gpsimd.tensor_scalar(neg_target[:], target[:], -1.0, 0.0, ALU.mult, ALU.add)
+
+        xa_words = tile([P, J], U32, "xa_words")
+        xa_scales = tile([P, J], U8, "xa_scales")
+        xb_words = tile([P, I], U32, "xb_words")
+        xb_scales = tile([P, I], U8, "xb_scales")
+        nc.vector.tensor_copy(xa_words[:], x_words[:].indirect(list_a[:]))
+        nc.vector.tensor_copy(xa_scales[:], x_scales[:].indirect(list_a[:]))
+        nc.vector.tensor_copy(xb_words[:], x_words[:].indirect(list_b[:]))
+        nc.vector.tensor_copy(xb_scales[:], x_scales[:].indirect(list_b[:]))
+
+        za = [psum.tile([P, 2, J], F32, name=f"za{u}") for u in range(2)]
+        for t in range(4):
+            cols = slice(P * t, P * (t + 1))
+            nc.tensor.matmul_mx(
+                out=za[t // 2][:, t % 2, :],
+                lhsT=wa_dealt[:, cols].bitcast(E5M2),
+                lhsT_scale=wa_scales_dealt[:, cols],
+                rhs=xa_words[:].bitcast(E4M3),
+                rhs_scale=xa_scales[:],
+                start=True,
+                stop=True,
+            )
+        zb = [psum.tile([P, 4, P], F32, name=f"zb{h}") for h in range(2)]
+        for h in range(2):
+            picks = slice(P * h, P * (h + 1))
+            for t in range(4):
+                nc.tensor.matmul_mx(
+                    out=zb[h][:, t, :],
+                    lhsT=wb_dealt[:, 2 * P * t : 2 * P * (t + 1)].bitcast(E2M1),
+                    lhsT_scale=wb_scales_dealt[:, P * t : P * (t + 1)],
+                    rhs=xb_words[:, picks].bitcast(E4M3),
+                    rhs_scale=xb_scales[:, picks],
+                    start=True,
+                    stop=True,
+                )
+
+        peak = [tile([P, 2], F32, f"peak{u}") for u in range(2)]
+        for u in range(2):
+            nc.vector.tensor_reduce(peak[u][:], za[u][:], AXIS_X, ALU.max)
+        above = tile([P, 2, J, 2], F32, "above")
+        for u in range(2):
+            nc.vector.scalar_tensor_tensor(
+                out=above[:, u, :, :],
+                in0=peak[u][:].unsqueeze(1).to_broadcast([P, J, 2]),
+                scalar=-0.4,
+                in1=za[u][:].rearrange("p e j -> p j e"),
+                op0=ALU.mult,
+                op1=ALU.add,
+            )
+
+        hb = tile([P, I, 4], BF16, "hb")
+        for h in range(2):
+            nc.scalar.activation(
+                out=hb[:, P * h : P * (h + 1), :], in_=zb[h][:].rearrange("p t i -> p i t"), func=RELU
+            )
+        hb_words = tile([P, I], U32, "hb_words")
+        hb_scales = tile([P, I], U8, "hb_scales")
+
+        ha = [tile([P, P, 4], BF16, f"ha{h}") for h in range(2)]
+        ha_words = [tile([P, P], U32, f"ha_words{h}") for h in range(2)]
+        ha_scales = [tile([P, P], U8, f"ha_scales{h}") for h in range(2)]
+
+        def pairs(h):
+            return above[:, :, P * h : P * (h + 1), :].rearrange("p u j e -> p j u e")
+
+        def quantise_ha(h):
+            nc.vector.quantize_mx(
+                out=ha_words[h][:].bitcast(E4M3),
+                scales=ha_scales[h][:],
+                in_=ha[h][:].rearrange("p j t -> p (j t)"),
+            )
+
+        nc.vector.tensor_scalar_max(ha[0][:].rearrange("p j (u e) -> p j u e", u=2), pairs(0), 0.0)
+        nc.scalar.activation(out=ha[1][:].rearrange("p j (u e) -> p j u e", u=2), in_=pairs(1), func=RELU)
+        nc.vector.quantize_mx(
+            out=hb_words[:].bitcast(E5M2), scales=hb_scales[:], in_=hb[:].rearrange("p i t -> p (i t)")
+        )
+        quantise_ha(0)
+        quantise_ha(1)
+
+        for h in range(2):
+            score = psum.tile([P, I], F32, name=f"score{h}")
+            nc.tensor.matmul_mx(
+                out=score[:],
+                lhsT=ha_words[h][:].bitcast(E4M3),
+                lhsT_scale=ha_scales[h][:],
+                rhs=hb_words[:].bitcast(E5M2),
+                rhs_scale=hb_scales[:],
+                start=True,
+                stop=True,
+            )
+            excess = tile([P, I], F32, f"excess{h}")
+            nc.scalar.activation(out=excess[:], in_=score[:], func=RELU, bias=neg_target[:, h : h + 1])
+            result = tile([P, I], F32, f"result{h}")
+            nc.vector.scalar_tensor_tensor(
+                out=result[:], in0=excess[:], scalar=0.04, in1=col_weight[:], op0=ALU.mult, op1=ALU.mult
+            )
+            nc.sync.dma_start(out=out[P * h : P * (h + 1), :], in_=result[:])

@@ -21,12 +21,15 @@ AXIS_X = mybir.AxisListType.X
 P = 128
 
 
-def load_scales(queues, plane, scales):
-    for q in range(4):
-        queues[q].dma_start(
-            out=plane[32 * q : 32 * q + 4, :].bitcast(I32),
-            in_=scales[0, 4 * q : 4 * q + 4, :].bitcast(I32),
-        )
+def load_scale_head(queue, plane, scales):
+    queue.dma_start(out=plane[0:2, :].bitcast(I32), in_=scales[0].bitcast(I32)[0:2, :])
+
+
+def load_scale_rest(queue, plane, scales):
+    queue.dma_start(
+        out=plane[2:P, :].bitcast(I32),
+        in_=scales[0].bitcast(I32)[2:16, :].unsqueeze(0).to_broadcast([9, 14, R // 4]),
+    )
 
 
 def deal(engine_copy, dealt, raw):
@@ -44,8 +47,8 @@ def tile_list_meet_peakgated_plain_hinge_kernel(
         pool = ctx.enter_context(tc.tile_pool(name="keep", bufs=1))
         psum = ctx.enter_context(tc.psum_pool(name="psum", bufs=1))
 
-        def tile(shape, dtype, name):
-            return pool.tile(shape, dtype, name=name, align_bytes=64)
+        def tile(shape, dtype, name, tag=None):
+            return pool.tile(shape, dtype, name=name, tag=tag or name, align_bytes=64)
 
         list_a = pool.tile([P, J // 16], U16, name="list_a")
         list_b = pool.tile([P, I // 16], U16, name="list_b")
@@ -55,28 +58,18 @@ def tile_list_meet_peakgated_plain_hinge_kernel(
         wa_scales_raw = tile([P, R], U8, "wa_scales_raw")
         wb_raw = tile([P, R // 2], U32, "wb_raw")
         wb_scales_raw = tile([P, R], U8, "wb_scales_raw")
-        target = tile([P, 2], F32, "target")
-        col_weight = tile([P, I], F32, "col_weight")
-
-        nc.vector.memset(x_scales[:].bitcast(I32), 0)
-        nc.vector.memset(wa_scales_raw[:].bitcast(I32), 0)
-        nc.vector.memset(wb_scales_raw[:].bitcast(I32), 0)
 
         nc.sync.dma_start(list_a[:], offs)
-        nc.sync.dma_start(
-            out=x_words[:].bitcast(I32), in_=xt_words[0].rearrange("p n t -> p (n t)").bitcast(I32)
-        )
-        nc.scalar.dma_start(
-            out=wa_raw[:].bitcast(I32), in_=wa_words[0].rearrange("p n t -> p (n t)").bitcast(I32)
-        )
-        load_scales([nc.sync] * 4, x_scales, xt_scales)
+        load_scale_rest(nc.scalar, x_scales, xt_scales)
+        nc.sync.dma_start(out=x_words[:].bitcast(I32), in_=xt_words[0].rearrange("p n t -> p (n t)").bitcast(I32))
+        nc.scalar.dma_start(out=wa_raw[:].bitcast(I32), in_=wa_words[0].rearrange("p n t -> p (n t)").bitcast(I32))
+        load_scale_head(nc.sync, x_scales, xt_scales)
+        load_scale_head(nc.sync, wa_scales_raw, wa_scales)
+        load_scale_rest(nc.sync, wa_scales_raw, wa_scales)
         nc.sync.dma_start(list_b[:], offs2)
-        load_scales([nc.sync] * 4, wa_scales_raw, wa_scales)
         nc.sync.dma_start(out=wb_raw[:].bitcast(I32), in_=wb_words[0].bitcast(I32))
-        load_scales([nc.sync, nc.sync, nc.sync, nc.gpsimd], wb_scales_raw, wb_scales)
-        with nc.allow_non_contiguous_dma(reason="one target for each partition"):
-            nc.sync.dma_start(out=target[:], in_=tg.rearrange("(h p) o -> p (h o)", p=P))
-        nc.sync.dma_start(out=col_weight[:], in_=cw1[0].partition_broadcast(P))
+        load_scale_rest(nc.gpsimd, wb_scales_raw, wb_scales)
+        load_scale_head(nc.gpsimd, wb_scales_raw, wb_scales)
 
         wa_dealt = tile([P, R], U32, "wa_dealt")
         wa_scales_dealt = tile([P, R], U8, "wa_scales_dealt")
@@ -86,9 +79,6 @@ def tile_list_meet_peakgated_plain_hinge_kernel(
         deal(nc.scalar.copy, wa_scales_dealt[:].bitcast(U32), wa_scales_raw[:].bitcast(U32))
         deal(nc.scalar.copy, wb_dealt[:].bitcast(U32), wb_raw[:])
         deal(nc.scalar.copy, wb_scales_dealt[:].bitcast(U32), wb_scales_raw[:].bitcast(U32))
-
-        neg_target = tile([P, 2], F32, "neg_target")
-        nc.gpsimd.tensor_scalar(neg_target[:], target[:], -1.0, 0.0, ALU.mult, ALU.add)
 
         xa_words = tile([P, J], U32, "xa_words")
         xa_scales = tile([P, J], U8, "xa_scales")
@@ -125,6 +115,14 @@ def tile_list_meet_peakgated_plain_hinge_kernel(
                     stop=True,
                 )
 
+        target = tile([P, 2], F32, "target", tag="xa_words")
+        with nc.allow_non_contiguous_dma(reason="one target for each partition"):
+            nc.sync.dma_start(out=target[:], in_=tg.rearrange("(h p) o -> p (h o)", p=P))
+        col_weight = tile([P, I], F32, "col_weight", tag="wa_raw")
+        nc.sync.dma_start(out=col_weight[:], in_=cw1[0].partition_broadcast(P))
+        neg_target = tile([P, 2], F32, "neg_target")
+        nc.gpsimd.tensor_scalar(neg_target[:], target[:], -1.0, 0.0, ALU.mult, ALU.add)
+
         peak = [tile([P, 2], F32, f"peak{u}") for u in range(2)]
         for u in range(2):
             nc.vector.tensor_reduce(peak[u][:], za[u][:], AXIS_X, ALU.max)
@@ -147,7 +145,7 @@ def tile_list_meet_peakgated_plain_hinge_kernel(
         hb_words = tile([P, I], U32, "hb_words")
         hb_scales = tile([P, I], U8, "hb_scales")
 
-        ha = [tile([P, P, 4], BF16, f"ha{h}") for h in range(2)]
+        ha = [tile([P, P, 4], BF16, "ha0"), tile([P, P, 4], BF16, "ha1", tag="wb_dealt")]
         ha_words = [tile([P, P], U32, f"ha_words{h}") for h in range(2)]
         ha_scales = [tile([P, P], U8, f"ha_scales{h}") for h in range(2)]
 

@@ -58,6 +58,8 @@ def tile_list_meet_peakgated_plain_hinge_kernel(
         wa_scales_raw = tile([P, R], U8, "wa_scales_raw")
         wb_raw = tile([P, R // 2], U32, "wb_raw")
         wb_scales_raw = tile([P, R], U8, "wb_scales_raw")
+        target = tile([P, 2], F32, "target")
+        col_weight = tile([P, I], F32, "col_weight")
 
         nc.sync.dma_start(list_a[:], offs)
         load_scale_rest(nc.scalar, x_scales, xt_scales)
@@ -70,6 +72,9 @@ def tile_list_meet_peakgated_plain_hinge_kernel(
         nc.sync.dma_start(out=wb_raw[:].bitcast(I32), in_=wb_words[0].bitcast(I32))
         load_scale_rest(nc.gpsimd, wb_scales_raw, wb_scales)
         load_scale_head(nc.gpsimd, wb_scales_raw, wb_scales)
+        with nc.allow_non_contiguous_dma(reason="one target for each partition"):
+            nc.sync.dma_start(out=target[:], in_=tg.rearrange("(h p) o -> p (h o)", p=P))
+        nc.sync.dma_start(out=col_weight[:], in_=cw1[0].partition_broadcast(P))
 
         wa_dealt = tile([P, R], U32, "wa_dealt")
         wa_scales_dealt = tile([P, R], U8, "wa_scales_dealt")
@@ -79,6 +84,9 @@ def tile_list_meet_peakgated_plain_hinge_kernel(
         deal(nc.scalar.copy, wa_scales_dealt[:].bitcast(U32), wa_scales_raw[:].bitcast(U32))
         deal(nc.scalar.copy, wb_dealt[:].bitcast(U32), wb_raw[:])
         deal(nc.scalar.copy, wb_scales_dealt[:].bitcast(U32), wb_scales_raw[:].bitcast(U32))
+
+        neg_target = tile([P, 2], F32, "neg_target")
+        nc.gpsimd.tensor_scalar(neg_target[:], target[:], -1.0, 0.0, ALU.mult, ALU.add)
 
         xa_words = tile([P, J], U32, "xa_words")
         xa_scales = tile([P, J], U8, "xa_scales")
@@ -115,27 +123,20 @@ def tile_list_meet_peakgated_plain_hinge_kernel(
                     stop=True,
                 )
 
-        target = tile([P, 2], F32, "target", tag="xa_words")
-        with nc.allow_non_contiguous_dma(reason="one target for each partition"):
-            nc.sync.dma_start(out=target[:], in_=tg.rearrange("(h p) o -> p (h o)", p=P))
-        col_weight = tile([P, I], F32, "col_weight", tag="wa_raw")
-        nc.sync.dma_start(out=col_weight[:], in_=cw1[0].partition_broadcast(P))
-        neg_target = tile([P, 2], F32, "neg_target")
-        nc.gpsimd.tensor_scalar(neg_target[:], target[:], -1.0, 0.0, ALU.mult, ALU.add)
-
         peak = [tile([P, 2], F32, f"peak{u}") for u in range(2)]
         for u in range(2):
             nc.vector.tensor_reduce(peak[u][:], za[u][:], AXIS_X, ALU.max)
-        above = tile([P, 2, J, 2], F32, "above")
-        for u in range(2):
-            nc.vector.scalar_tensor_tensor(
-                out=above[:, u, :, :],
-                in0=peak[u][:].unsqueeze(1).to_broadcast([P, J, 2]),
-                scalar=-0.4,
-                in1=za[u][:].rearrange("p e j -> p j e"),
-                op0=ALU.mult,
-                op1=ALU.add,
-            )
+        above = [tile([P, 2, P, 2], F32, f"above{h}") for h in range(2)]
+        for h in range(2):
+            for u in range(2):
+                nc.vector.scalar_tensor_tensor(
+                    out=above[h][:, u, :, :],
+                    in0=peak[u][:].unsqueeze(1).to_broadcast([P, P, 2]),
+                    scalar=-0.4,
+                    in1=za[u][:, :, P * h : P * (h + 1)].rearrange("p e j -> p j e"),
+                    op0=ALU.mult,
+                    op1=ALU.add,
+                )
 
         hb = tile([P, I, 4], BF16, "hb")
         for h in range(2):
@@ -145,12 +146,12 @@ def tile_list_meet_peakgated_plain_hinge_kernel(
         hb_words = tile([P, I], U32, "hb_words")
         hb_scales = tile([P, I], U8, "hb_scales")
 
-        ha = [tile([P, P, 4], BF16, "ha0"), tile([P, P, 4], BF16, "ha1", tag="wb_dealt")]
+        ha = [tile([P, P, 4], BF16, "ha0", tag="wb_dealt"), tile([P, P, 4], BF16, "ha1")]
         ha_words = [tile([P, P], U32, f"ha_words{h}") for h in range(2)]
         ha_scales = [tile([P, P], U8, f"ha_scales{h}") for h in range(2)]
 
         def pairs(h):
-            return above[:, :, P * h : P * (h + 1), :].rearrange("p u j e -> p j u e")
+            return above[h][:].rearrange("p u j e -> p j u e")
 
         def quantise_ha(h):
             nc.vector.quantize_mx(
@@ -159,29 +160,36 @@ def tile_list_meet_peakgated_plain_hinge_kernel(
                 in_=ha[h][:].rearrange("p j t -> p (j t)"),
             )
 
-        nc.vector.tensor_scalar_max(ha[0][:].rearrange("p j (u e) -> p j u e", u=2), pairs(0), 0.0)
-        nc.scalar.activation(out=ha[1][:].rearrange("p j (u e) -> p j u e", u=2), in_=pairs(1), func=RELU)
+        nc.scalar.activation(out=ha[0][:].rearrange("p j (u e) -> p j u e", u=2), in_=pairs(0), func=RELU)
         nc.vector.quantize_mx(
             out=hb_words[:].bitcast(E5M2), scales=hb_scales[:], in_=hb[:].rearrange("p i t -> p (i t)")
         )
+        nc.vector.tensor_scalar_max(ha[1][:].rearrange("p j (u e) -> p j u e", u=2), pairs(1), 0.0)
         quantise_ha(0)
         quantise_ha(1)
 
         for h in range(2):
-            score = psum.tile([P, I], F32, name=f"score{h}")
-            nc.tensor.matmul_mx(
-                out=score[:],
-                lhsT=ha_words[h][:].bitcast(E4M3),
-                lhsT_scale=ha_scales[h][:],
-                rhs=hb_words[:].bitcast(E5M2),
-                rhs_scale=hb_scales[:],
-                start=True,
-                stop=True,
-            )
-            excess = tile([P, I], F32, f"excess{h}")
-            nc.scalar.activation(out=excess[:], in_=score[:], func=RELU, bias=neg_target[:, h : h + 1])
             result = tile([P, I], F32, f"result{h}")
-            nc.vector.scalar_tensor_tensor(
-                out=result[:], in0=excess[:], scalar=0.04, in1=col_weight[:], op0=ALU.mult, op1=ALU.mult
-            )
+            for g in range(2):
+                cols = slice(P * g, P * (g + 1))
+                score = psum.tile([P, P], F32, name=f"score{h}{g}")
+                nc.tensor.matmul_mx(
+                    out=score[:],
+                    lhsT=ha_words[h][:].bitcast(E4M3),
+                    lhsT_scale=ha_scales[h][:],
+                    rhs=hb_words[:, cols].bitcast(E5M2),
+                    rhs_scale=hb_scales[:, cols],
+                    start=True,
+                    stop=True,
+                )
+                excess = tile([P, P], F32, f"excess{h}{g}")
+                nc.scalar.activation(out=excess[:], in_=score[:], func=RELU, bias=neg_target[:, h : h + 1])
+                nc.vector.scalar_tensor_tensor(
+                    out=result[:, cols],
+                    in0=excess[:],
+                    scalar=0.04,
+                    in1=col_weight[:, cols],
+                    op0=ALU.mult,
+                    op1=ALU.mult,
+                )
             nc.sync.dma_start(out=out[P * h : P * (h + 1), :], in_=result[:])

@@ -76,12 +76,15 @@ def tile_list_meet_peakgated_plain_hinge_kernel(
             nc.sync.dma_start(out=target[:], in_=tg.rearrange("(h p) o -> p (h o)", p=P))
         nc.sync.dma_start(out=col_weight[:], in_=cw1[0].partition_broadcast(P))
 
-        wa_dealt = tile([P, R], U32, "wa_dealt")
+        wa_dealt = [tile([P, R // 2], U32, f"wa_dealt{u}") for u in range(2)]
         wa_scales_dealt = tile([P, R], U8, "wa_scales_dealt")
         wb_dealt = tile([P, 2 * R], U8, "wb_dealt")
         wb_scales_dealt = tile([P, R], U8, "wb_scales_dealt")
-        deal(nc.scalar.copy, wa_dealt[:], wa_raw[:])
-        deal(nc.scalar.copy, wa_scales_dealt[:].bitcast(U32), wa_scales_raw[:].bitcast(U32))
+        for u in range(2):
+            nc.scalar.copy(
+                out=wa_dealt[u][:].rearrange("p (t b q) -> p t b q", t=2, b=16),
+                in_=wa_raw[:].rearrange("p (b t q) -> p t b q", t=4, b=16)[:, 2 * u : 2 * u + 2, :, :],
+            )
         deal(nc.scalar.copy, wb_dealt[:].bitcast(U32), wb_raw[:])
         deal(nc.scalar.copy, wb_scales_dealt[:].bitcast(U32), wb_scales_raw[:].bitcast(U32))
 
@@ -94,6 +97,7 @@ def tile_list_meet_peakgated_plain_hinge_kernel(
         xb_scales = tile([P, I], U8, "xb_scales")
         nc.vector.tensor_copy(xa_words[:], x_words[:].indirect(list_a[:]))
         nc.vector.tensor_copy(xa_scales[:], x_scales[:].indirect(list_a[:]))
+        deal(nc.vector.tensor_copy, wa_scales_dealt[:].bitcast(I32), wa_scales_raw[:].bitcast(I32))
         nc.vector.tensor_copy(xb_words[:], x_words[:].indirect(list_b[:]))
         nc.vector.tensor_copy(xb_scales[:], x_scales[:].indirect(list_b[:]))
 
@@ -102,7 +106,7 @@ def tile_list_meet_peakgated_plain_hinge_kernel(
             cols = slice(P * t, P * (t + 1))
             nc.tensor.matmul_mx(
                 out=za[t // 2][:, t % 2, :],
-                lhsT=wa_dealt[:, cols].bitcast(E5M2),
+                lhsT=wa_dealt[t // 2][:, P * (t % 2) : P * (t % 2 + 1)].bitcast(E5M2),
                 lhsT_scale=wa_scales_dealt[:, cols],
                 rhs=xa_words[:].bitcast(E4M3),
                 rhs_scale=xa_scales[:],
@@ -183,7 +187,10 @@ def tile_list_meet_peakgated_plain_hinge_kernel(
                     stop=True,
                 )
                 excess = tile([P, P], F32, f"excess{h}{g}")
-                nc.scalar.activation(out=excess[:], in_=score[:], func=RELU, bias=neg_target[:, h : h + 1])
+                if h == 0 and g == 0:
+                    nc.vector.tensor_scalar(excess[:], score[:], target[:, 0:1], 0.0, ALU.subtract, ALU.max)
+                else:
+                    nc.scalar.activation(out=excess[:], in_=score[:], func=RELU, bias=neg_target[:, h : h + 1])
                 nc.vector.scalar_tensor_tensor(
                     out=result[:, cols],
                     in0=excess[:],

from contextlib import ExitStack

import concourse.mybir as mybir

K, T, J, I, R = 512, 512, 256, 256, 512
FLOPS = 2 * K * R * J + 2 * K * R * I + 2 * R * J * I

F32 = mybir.dt.float32
BF16 = mybir.dt.bfloat16
I32 = mybir.dt.int32
U32 = mybir.dt.uint32
U16 = mybir.dt.uint16
U8 = mybir.dt.uint8
E4M3 = mybir.dt.float8_e4m3fn_x4
E5M2 = mybir.dt.float8_e5m2_x4
E2M1 = mybir.dt.float4_e2m1fn_x4
ALU = mybir.AluOpType
RELU = mybir.ActivationFunctionType.Relu
AXIS_X = mybir.AxisListType.X

P = 128


def load_scale_head(queue, plane, scales):
    queue.dma_start(out=plane[0:2, :].bitcast(I32), in_=scales[0].bitcast(I32)[0:2, :])


def load_scale_rest(queue, plane, scales):
    queue.dma_start(
        out=plane[2:P, :].bitcast(I32),
        in_=scales[0].bitcast(I32)[2:16, :].unsqueeze(0).to_broadcast([9, 14, R // 4]),
    )


def deal(engine_copy, dealt, raw):
    engine_copy(
        out=dealt.rearrange("p (t b q) -> p t b q", t=4, b=16),
        in_=raw.rearrange("p (b t q) -> p t b q", t=4, b=16),
    )


def tile_list_meet_peakgated_plain_hinge_kernel(
    tc, xt_words, xt_scales, wa_words, wa_scales, wb_words, wb_scales, tg, cw1, offs, offs2, out
):
    nc = tc.nc
    with ExitStack() as ctx:
        pool = ctx.enter_context(tc.tile_pool(name="keep", bufs=1))
        psum = ctx.enter_context(tc.psum_pool(name="psum", bufs=1))

        def tile(shape, dtype, name, tag=None):
            return pool.tile(shape, dtype, name=name, tag=tag or name, align_bytes=64)

        list_a = pool.tile([P, J // 16], U16, name="list_a")
        list_b = pool.tile([P, I // 16], U16, name="list_b")
        x_words = tile([P, T], U32, "x_words")
        x_scales = tile([P, T], U8, "x_scales")
        wa_raw = tile([P, R], U32, "wa_raw")
        wa_scales_raw = tile([P, R], U8, "wa_scales_raw")
        wb_raw = tile([P, R // 2], U32, "wb_raw")
        wb_scales_raw = tile([P, R], U8, "wb_scales_raw")
        target = tile([P, 2], F32, "target")
        col_weight = tile([P, I], F32, "col_weight")

        nc.sync.dma_start(list_a[:], offs)
        load_scale_rest(nc.scalar, x_scales, xt_scales)
        nc.sync.dma_start(out=x_words[:].bitcast(I32), in_=xt_words[0].rearrange("p n t -> p (n t)").bitcast(I32))
        nc.scalar.dma_start(out=wa_raw[:].bitcast(I32), in_=wa_words[0].rearrange("p n t -> p (n t)").bitcast(I32))
        load_scale_head(nc.sync, x_scales, xt_scales)
        load_scale_head(nc.sync, wa_scales_raw, wa_scales)
        load_scale_rest(nc.sync, wa_scales_raw, wa_scales)
        nc.sync.dma_start(list_b[:], offs2)
        nc.sync.dma_start(out=wb_raw[:].bitcast(I32), in_=wb_words[0].bitcast(I32))
        load_scale_rest(nc.gpsimd, wb_scales_raw, wb_scales)
        load_scale_head(nc.gpsimd, wb_scales_raw, wb_scales)
        with nc.allow_non_contiguous_dma(reason="one target for each partition"):
            nc.sync.dma_start(out=target[:], in_=tg.rearrange("(h p) o -> p (h o)", p=P))
        nc.sync.dma_start(out=col_weight[:], in_=cw1[0].partition_broadcast(P))

        wa_dealt = [tile([P, R // 2], U32, f"wa_dealt{u}") for u in range(2)]
        wa_scales_dealt = tile([P, R], U8, "wa_scales_dealt")
        wb_dealt = tile([P, 2 * R], U8, "wb_dealt")
        wb_scales_dealt = tile([P, R], U8, "wb_scales_dealt")
        for u in range(2):
            nc.scalar.copy(
                out=wa_dealt[u][:].rearrange("p (t b q) -> p t b q", t=2, b=16),
                in_=wa_raw[:].rearrange("p (b t q) -> p t b q", t=4, b=16)[:, 2 * u : 2 * u + 2, :, :],
            )
        deal(nc.scalar.copy, wb_dealt[:].bitcast(U32), wb_raw[:])
        deal(nc.scalar.copy, wb_scales_dealt[:].bitcast(U32), wb_scales_raw[:].bitcast(U32))

        neg_target = tile([P, 2], F32, "neg_target")
        nc.gpsimd.tensor_scalar(neg_target[:], target[:], -1.0, 0.0, ALU.mult, ALU.add)

        xa_words = tile([P, J], U32, "xa_words")
        xa_scales = tile([P, J], U8, "xa_scales")
        xb_words = tile([P, I], U32, "xb_words")
        xb_scales = tile([P, I], U8, "xb_scales")
        nc.vector.tensor_copy(xa_words[:], x_words[:].indirect(list_a[:]))
        nc.vector.tensor_copy(xa_scales[:], x_scales[:].indirect(list_a[:]))
        deal(nc.vector.tensor_copy, wa_scales_dealt[:].bitcast(I32), wa_scales_raw[:].bitcast(I32))
        nc.vector.tensor_copy(xb_words[:], x_words[:].indirect(list_b[:]))
        nc.vector.tensor_copy(xb_scales[:], x_scales[:].indirect(list_b[:]))

        za = [psum.tile([P, 2, J], F32, name=f"za{u}") for u in range(2)]
        for t in range(4):
            cols = slice(P * t, P * (t + 1))
            nc.tensor.matmul_mx(
                out=za[t // 2][:, t % 2, :],
                lhsT=wa_dealt[t // 2][:, P * (t % 2) : P * (t % 2 + 1)].bitcast(E5M2),
                lhsT_scale=wa_scales_dealt[:, cols],
                rhs=xa_words[:].bitcast(E4M3),
                rhs_scale=xa_scales[:],
                start=True,
                stop=True,
            )
        zb = [psum.tile([P, 4, P], F32, name=f"zb{h}") for h in range(2)]
        for h in range(2):
            picks = slice(P * h, P * (h + 1))
            for t in range(4):
                nc.tensor.matmul_mx(
                    out=zb[h][:, t, :],
                    lhsT=wb_dealt[:, 2 * P * t : 2 * P * (t + 1)].bitcast(E2M1),
                    lhsT_scale=wb_scales_dealt[:, P * t : P * (t + 1)],
                    rhs=xb_words[:, picks].bitcast(E4M3),
                    rhs_scale=xb_scales[:, picks],
                    start=True,
                    stop=True,
                )

        peak = [tile([P, 2], F32, f"peak{u}") for u in range(2)]
        for u in range(2):
            nc.vector.tensor_reduce(peak[u][:], za[u][:], AXIS_X, ALU.max)
        above = [tile([P, 2, P, 2], F32, f"above{h}") for h in range(2)]
        for h in range(2):
            for u in range(2):
                nc.vector.scalar_tensor_tensor(
                    out=above[h][:, u, :, :],
                    in0=peak[u][:].unsqueeze(1).to_broadcast([P, P, 2]),
                    scalar=-0.4,
                    in1=za[u][:, :, P * h : P * (h + 1)].rearrange("p e j -> p j e"),
                    op0=ALU.mult,
                    op1=ALU.add,
                )

        hb = tile([P, I, 4], BF16, "hb")
        for h in range(2):
            nc.scalar.activation(
                out=hb[:, P * h : P * (h + 1), :], in_=zb[h][:].rearrange("p t i -> p i t"), func=RELU
            )
        hb_words = tile([P, I], U32, "hb_words")
        hb_scales = tile([P, I], U8, "hb_scales")

        ha = [tile([P, P, 4], BF16, "ha0", tag="wb_dealt"), tile([P, P, 4], BF16, "ha1")]
        ha_words = [tile([P, P], U32, f"ha_words{h}") for h in range(2)]
        ha_scales = [tile([P, P], U8, f"ha_scales{h}") for h in range(2)]

        def pairs(h):
            return above[h][:].rearrange("p u j e -> p j u e")

        def quantise_ha(h):
            nc.vector.quantize_mx(
                out=ha_words[h][:].bitcast(E4M3),
                scales=ha_scales[h][:],
                in_=ha[h][:].rearrange("p j t -> p (j t)"),
            )

        nc.scalar.activation(out=ha[0][:].rearrange("p j (u e) -> p j u e", u=2), in_=pairs(0), func=RELU)
        nc.vector.quantize_mx(
            out=hb_words[:].bitcast(E5M2), scales=hb_scales[:], in_=hb[:].rearrange("p i t -> p (i t)")
        )
        nc.vector.tensor_scalar_max(ha[1][:].rearrange("p j (u e) -> p j u e", u=2), pairs(1), 0.0)
        quantise_ha(0)
        quantise_ha(1)

        for h in range(2):
            result = tile([P, I], F32, f"result{h}")
            for g in range(2):
                cols = slice(P * g, P * (g + 1))
                score = psum.tile([P, P], F32, name=f"score{h}{g}")
                nc.tensor.matmul_mx(
                    out=score[:],
                    lhsT=ha_words[h][:].bitcast(E4M3),
                    lhsT_scale=ha_scales[h][:],
                    rhs=hb_words[:, cols].bitcast(E5M2),
                    rhs_scale=hb_scales[:, cols],
                    start=True,
                    stop=True,
                )
                excess = tile([P, P], F32, f"excess{h}{g}")
                if h == 0 and g == 0:
                    nc.vector.tensor_scalar(excess[:], score[:], target[:, 0:1], 0.0, ALU.subtract, ALU.max)
                else:
                    nc.scalar.activation(out=excess[:], in_=score[:], func=RELU, bias=neg_target[:, h : h + 1])
                nc.vector.scalar_tensor_tensor(
                    out=result[:, cols],
                    in0=excess[:],
                    scalar=0.04,
                    in1=col_weight[:, cols],
                    op0=ALU.mult,
                    op1=ALU.mult,
                )
            nc.sync.dma_start(out=out[P * h : P * (h + 1), :], in_=result[:])
